import numpy as np, ml_dtypes
CORES = [5,13,29,37,53,69,77,101,133,141,157,165,181,197,205,229]
N = 16
KT, HT, TK = 1, 4, 128
def setup_inputs(rng):
    w = (rng.standard_normal((128, KT * HT * 128), dtype=np.float32) / 8).astype(ml_dtypes.bfloat16)
    return {"x": rng.standard_normal((N, 128, KT * TK), dtype=np.float32).astype(ml_dtypes.bfloat16), "w": np.broadcast_to(w, (N,) + w.shape).copy()}
def setup_inputs_big(rng):
    d = setup_inputs(rng)
    for k in ("x", "w"): d[k] = (d[k].astype(np.float32) * 1024.0).astype(d[k].dtype)
    return d
def setup_inputs_small(rng):
    d = setup_inputs(rng)
    for k in ("x", "w"): d[k] = (d[k].astype(np.float32) * (1 / 1024.0)).astype(d[k].dtype)
    return d
def setup_inputs_apart(rng):
    d = setup_inputs(rng)
    f = (10.0 ** rng.permutation(np.linspace(-1.5, 1.5, N))).astype(np.float32).reshape(N, 1, 1)
    for k in ("x",): d[k] = (d[k].astype(np.float32) * f).astype(d[k].dtype)
    return d
def tie_inputs(x):
    x = dict(x)
    x["w"] = np.broadcast_to(x["w"][0], x["w"].shape).copy()
    return x
def reference(x, w):
    X, W = x.astype(np.float64), w.astype(np.float64)
    def hidden(r):
        return np.stack([np.maximum(sum(W[r][:, 128 * (HT * t + u):128 * (HT * t + u) + 128].T @ X[r][:, TK * t:TK * t + TK] for t in range(KT)), 0.0) for u in range(HT)])
    h = [hidden(r) for r in range(N)]
    y = np.stack([sum(h[(r - 1) % N][u].T @ h[r][u] for u in range(HT)) for r in range(N)])
    return {"y": y.astype(ml_dtypes.bfloat16 if x.dtype != np.float64 else np.float64)}

from concourse.mybir import AluOpType

N = 16
WORLD = 256
HT = 4
TK = 128

HOP1_ENGINES = 4

SCRATCH = {
    "xd": ("dram", [128, TK], "bfloat16"),
    "xs": ("sbuf", [128, TK], "bfloat16"),
    "ws": ("sbuf", [128, HT * TK], "bfloat16"),
    "xp": ("sbuf", [128, TK], "bfloat16"),
    "zero": ("sbuf", [128, HT * TK], "float32"),
    "hr": ("sbuf", [128, HT * TK], "bfloat16"),
    "hp": ("sbuf", [128, HT * TK], "bfloat16"),
    "ys": ("sbuf", [128, TK], "bfloat16"),
    "pr": ("psum", [128, 512], "float32"),
    "pp0": ("psum", [128, 512], "float32"),
    "pp1": ("psum", [128, 512], "float32"),
    "pp2": ("psum", [128, 512], "float32"),
    "pp3": ("psum", [128, 512], "float32"),
    "py": ("psum", [128, TK], "float32"),
}
SEMAPHORES = ["ldd", "ldx", "ldw", "sent", "harr", "arr", "z", "mr", "hrdone",
              "mp0", "mp1", "mp2", "mp3", "hp0", "hp1", "hp2", "hp3", "ydone", "ysdone", "stored"]


def _count(mask):
    n = 0
    while mask:
        n += mask & 1
        mask >>= 1
    return n


def _some(mask, n):
    out, b = 0, 0
    while n > 0:
        if (mask >> b) & 1:
            out |= 1 << b
            n -= 1
        b += 1
    return out


def _route(T, topo, r):
    src, dst = T.cores[r], T.cores[(r + 1) % N]
    if topo.may_write(src, dst):
        return src, None, dst
    cands = [c for c in range(WORLD)
             if c != src and T.rank_of(c) is None
             and topo.host(c) == topo.host(src) and topo.chip(c) == topo.chip(src)
             and topo.may_write(c, dst)]
    cands.sort(key=lambda c: (topo.die(c) != topo.die(src), c))
    return src, cands[0], dst


def _send(g, T, topo, core, dst, out_ap, remote_sem, mask):
    rid, pid = topo.addr(dst, core)
    g.remote_dma(out_ap=out_ap, in_ap=T.xd[:], remote_sem=remote_sem, local_sem=T.sem.sent,
                 pid=pid, routing_id=rid, dma_engine_mask=mask)
    g.wait_ge(T.sem.sent, _count(mask))


def rank_program(g, core, T, topo):
    S = T.sem
    routes = [_route(T, topo, r) for r in range(N)]

    for src, via, dst in routes:
        if via == core:
            g.wait_ge(S.harr, HOP1_ENGINES)
            _send(g, T, topo, core, dst, T.xp[:], S.arr, topo.mask(core, dst))
            return

    rank = T.rank_of(core)
    if rank is None:
        return
    src, via, dst = routes[rank]
    psrc, pvia, pdst = routes[(rank - 1) % N]
    last = psrc if pvia is None else pvia
    arrive = _count(topo.mask(last, core))

    g.sync.dma_start(T.xd[:], T.x[:]).then_inc(S.ldd, 16)
    g.sync.dma_start(T.xs[:], T.x[:]).then_inc(S.ldx, 16)
    g.sync.dma_start(T.ws[:], T.w[:]).then_inc(S.ldw, 16)

    g.wait_ge(S.ldd, 16)
    if via is None:
        _send(g, T, topo, core, dst, T.xp[:], S.arr, topo.mask(core, dst))
    else:
        _send(g, T, topo, core, via, T.xd[:], S.harr, _some(topo.mask(core, via), HOP1_ENGINES))

    te, ve = g.tensor, g.vector
    pp = [T.pp0, T.pp1, T.pp2, T.pp3]
    mp = [S.mp0, S.mp1, S.mp2, S.mp3]
    hs = [S.hp0, S.hp1, S.hp2, S.hp3]

    def col(t, u):
        return t[:, u * TK:(u + 1) * TK]

    te.wait_ge(S.ldx, 16)
    te.wait_ge(S.ldw, 16)
    for u in range(HT):
        te.matmul(col(T.pr, u), col(T.ws, u), T.xs[:], True, True).then_inc(S.mr, 1)
    te.wait_ge(S.arr, arrive)
    for u in range(HT):
        te.matmul(pp[u][:, 0:TK], col(T.ws, u), T.xp[:], True, True).then_inc(mp[u], 1)
    te.wait_ge(S.hrdone, 1)
    for u in range(HT):
        te.wait_ge(hs[u], 1)
        te.matmul(T.py[:], col(T.hp, u), col(T.hr, u), u == 0, u == HT - 1).then_inc(S.ydone, 1)

    ve.memset(T.zero[:], 0.0).then_inc(S.z, 1)
    ve.wait_ge(S.z, 1)
    ve.wait_ge(S.mr, HT)
    ve.tensor_tensor(T.hr[:], T.pr[:], T.zero[:], AluOpType.max).then_inc(S.hrdone, 1)
    for u in range(HT):
        ve.wait_ge(mp[u], 1)
        ve.tensor_tensor(col(T.hp, u), pp[u][:, 0:TK], T.zero[:, 0:TK], AluOpType.max).then_inc(hs[u], 1)
    ve.wait_ge(S.ydone, HT)
    ve.tensor_copy(T.ys[:], T.py[:]).then_inc(S.ysdone, 1)

    g.sync.wait_ge(S.ysdone, 1)
    g.sync.dma_start(T.y[:], T.ys[:]).then_inc(S.stored, 16)
    g.sync.wait_ge(S.stored, 16)
